import numpy as np
import ml_dtypes


def mxq(x, axis, fmt="e4m3"):
    dtype, down = {"e4m3": (ml_dtypes.float8_e4m3fn, 7), "e5m2": (ml_dtypes.float8_e5m2, 14)}[fmt]
    v = np.moveaxis(np.asarray(x, np.float32).astype(ml_dtypes.bfloat16).astype(np.float64), axis, -1)
    blocks = v.reshape(v.shape[:-1] + (-1, 32))
    amax = np.abs(blocks).max(-1, keepdims=True)
    byte = np.maximum(np.where(amax > 0, np.frexp(amax)[1] - 1 + 127, 0) - down, 1)
    scale = np.exp2(byte - 127.0)
    codes = (blocks / scale).astype(np.float32).astype(dtype).astype(np.float64)
    return np.moveaxis((codes * scale).reshape(v.shape), -1, axis)


WIDE = False


def mx_kscale(k):
    if not WIDE:
        return np.ones(k)
    levels = np.array([10, -10, 5, -5, 0])
    if k % 512:
        return np.exp2(np.random.permutation(np.resize(levels, k // 32))).repeat(32)
    a = np.empty((k // 512, 16))
    for p in range(k // 512):
        a[p, :8] = np.random.permutation(np.resize(levels, 8))
        for g in range(8):
            far = levels[np.abs(levels - a[p, g]) >= 10]
            a[p, g + 8] = far[np.random.randint(len(far))]
    return np.exp2(a.ravel()).repeat(32)


def f64(x):
    return np.asarray(x).astype(np.float64)


def striped8(idx):
    return np.asarray(idx).reshape(8, -1, 16).transpose(0, 2, 1).reshape(128, -1).astype(np.uint16)


def unstriped8(offs):
    return offs.reshape(8, 16, -1).transpose(0, 2, 1).reshape(8, -1).astype(np.int64)


def pick8(x, idx, run):
    r = np.arange(len(x))
    return x[r[:, None], idx[r % (8 * run) // run]]


E2M1 = np.array([0.0, 0.5, 1.0, 1.5, 2.0, 3.0, 4.0, 6.0, -0.0, -0.5, -1.0, -1.5, -2.0, -3.0, -4.0, -6.0])


def pack_weight(w, fmt):
    k, n = w.shape
    w = f64(np.asarray(w, np.float32).astype(ml_dtypes.bfloat16)).reshape(k // 32, 32, n)
    amax = np.abs(w).max(1)
    if fmt == "e4m3":
        byte = np.frexp(amax)[1] - 1 + 127 - 7
    else:
        mant, ex = np.frexp(amax / 6.0)
        byte = np.where(mant > 0.5, ex, ex - 1) + 127
    byte = np.clip(np.where(amax > 0, byte, 1), 1, 254)
    scaled = (w * np.exp2(127.0 - byte)[:, None, :]).reshape(k, n).astype(np.float32)
    by_word = np.ascontiguousarray(scaled.reshape(k // 512, 128, 4, n).transpose(0, 1, 3, 2))
    if fmt == "e4m3":
        words = by_word.astype(ml_dtypes.float8_e4m3fn).view(np.uint8)
    else:
        c = by_word.astype(ml_dtypes.float4_e2m1fn).view(np.uint8) & 0xF
        words = (c[..., 0::2] | (c[..., 1::2] << 4)).reshape(k // 512, 128, 2 * n)
    return np.ascontiguousarray(words), np.ascontiguousarray(byte.astype(np.uint8).reshape(k // 512, 16, n))


def unpack_weight(words, scales, fmt):
    g, _, n = scales.shape
    words = np.ascontiguousarray(words).reshape(g, 128, n, -1)
    if fmt == "e4m3":
        vals = words.view(ml_dtypes.float8_e4m3fn).astype(np.float64)
    else:
        nib = np.empty((g, 128, n, 4), np.uint8)
        nib[..., 0::2] = words & 0xF
        nib[..., 1::2] = words >> 4
        vals = E2M1[nib]
    vals = vals * np.repeat(np.exp2(scales.astype(np.float64) - 127.0), 8, axis=1)[..., None]
    return vals.transpose(0, 1, 3, 2).reshape(g * 512, n)


D, T, U, X, S, I, Q = 512, 1024, 1024, 1024, 1024, 512, 128


def setup_inputs():
    n = np.random.standard_normal
    idx = np.stack([np.random.permutation(U)[:I] for _ in range(8)])
    idx2 = np.stack([np.random.permutation(T)[:I] for _ in range(8)])
    idx3 = np.stack([np.random.permutation(X)[:I] for _ in range(8)])
    idx4 = np.stack([np.random.permutation(T)[:I] for _ in range(8)])
    idx5 = np.stack([np.random.permutation(S)[:I] for _ in range(8)])
    idx6 = np.stack([np.random.permutation(T)[:I] for _ in range(8)])
    idx7 = np.stack([np.random.permutation(T)[:I] for _ in range(8)])
    fd = mx_kscale(D)
    cachep = pack_weight(n((D, T)) / fd[:, None], "e2m1")
    draftp = pack_weight(n((D, U)) / fd[:, None], "e4m3")
    archp = pack_weight(n((D, X)) / fd[:, None], "e2m1")
    prefp = pack_weight(n((D, S)) / fd[:, None], "e4m3")
    return {
        "query": (n((D, Q)) * 1.0 / np.sqrt(D) * fd[:, None]).astype(np.float32),
        "query2": (n((D, Q)) * 1.0 / np.sqrt(D) * fd[:, None]).astype(np.float32),
        "cache_words": cachep[0],
        "cache_scales": cachep[1],
        "draft_words": draftp[0],
        "draft_scales": draftp[1],
        "arch_words": archp[0],
        "arch_scales": archp[1],
        "pref_words": prefp[0],
        "pref_scales": prefp[1],
        "offs": striped8(idx),
        "offs2": striped8(idx2),
        "offs3": striped8(idx3),
        "offs4": striped8(idx4),
        "offs5": striped8(idx5),
        "offs6": striped8(idx6),
        "offs7": striped8(idx7),
    }


def reference(query, query2, cache_words, cache_scales, draft_words, draft_scales, arch_words, arch_scales, pref_words, pref_scales, offs, offs2, offs3, offs4, offs5, offs6, offs7):
    idx = unstriped8(offs)
    idx2 = unstriped8(offs2)
    idx3 = unstriped8(offs3)
    idx4 = unstriped8(offs4)
    idx5 = unstriped8(offs5)
    idx6 = unstriped8(offs6)
    idx7 = unstriped8(offs7)
    cacheu = unpack_weight(cache_words, cache_scales, "e2m1")
    draftu = unpack_weight(draft_words, draft_scales, "e4m3")
    archu = unpack_weight(arch_words, arch_scales, "e2m1")
    prefu = unpack_weight(pref_words, pref_scales, "e4m3")
    queryq = mxq(f64(query), 0, "e4m3")
    a = queryq.T @ cacheu
    b = queryq.T @ draftu
    query2q = mxq(f64(query2), 0, "e4m3")
    c0 = query2q.T @ archu
    d0 = query2q.T @ prefu
    f1 = np.zeros((Q, T))
    f1[np.arange(Q)[:, None], idx2[np.arange(Q) % 128 // 16]] = pick8(b, idx, 16)
    f2 = np.zeros((Q, T))
    f2[np.arange(Q)[:, None], idx4[np.arange(Q) % 128 // 16]] = pick8(c0, idx3, 16)
    f3 = np.zeros((Q, T))
    f3[np.arange(Q)[:, None], idx6[np.arange(Q) % 128 // 16]] = pick8(d0, idx5, 16)
    m1 = np.maximum(f1, f2)
    m2 = np.minimum(m1, f3)
    aa = a - m2
    y = pick8(aa, idx7, 16)
    return y

from contextlib import ExitStack

import concourse.mybir as mybir

D, TOKENS, SLOTS, ROWS = 512, 1024, 512, 128
FLOPS = 4 * 2 * D * ROWS * TOKENS

F32 = mybir.dt.float32
BF16 = mybir.dt.bfloat16
I32 = mybir.dt.int32
U32 = mybir.dt.uint32
U16 = mybir.dt.uint16
U8 = mybir.dt.uint8
FP8X4 = mybir.dt.float8_e4m3fn_x4
FP4X4 = mybir.dt.float4_e2m1fn_x4
COPY = mybir.ActivationFunctionType.Copy
ALU = mybir.AluOpType

P = 128
PACK = 4
BANK = 512
LIST_COLS = SLOTS // 16


def tile_attend_fourmeet_fourtwo_kernel(
    tc, query, query2, cache_words, cache_scales, draft_words, draft_scales, arch_words, arch_scales,
    pref_words, pref_scales, offs, offs2, offs3, offs4, offs5, offs6, offs7, out,
):
    nc = tc.nc
    with ExitStack() as ctx:
        lists = ctx.enter_context(tc.tile_pool(name="lists", bufs=1))
        keep = ctx.enter_context(tc.tile_pool(name="keep", bufs=1))
        psum = ctx.enter_context(tc.psum_pool(name="psum", bufs=1))

        def load_list(src, name):
            t = lists.tile([P, LIST_COLS], U16, name=name)
            nc.sync.dma_start(t[:], src)
            return t

        def load_query(src, name):
            raw = keep.tile([P, PACK, ROWS], F32, name=name + "_raw")
            nc.sync.dma_start(raw[:], src.rearrange("(p j) w -> p j w", j=PACK))
            return raw

        def load_words4(src, name):
            t = keep.tile([P, 2 * TOKENS], U8, name=name, align_bytes=256)
            nc.sync.dma_start(t[:].bitcast(I32), src[0].bitcast(I32))
            return t

        def load_words8(src, name):
            t = keep.tile([P, TOKENS], U32, name=name, align_bytes=256)
            nc.sync.dma_start(t[:].bitcast(I32), src[0].rearrange("p n t -> p (n t)").bitcast(I32))
            return t

        def load_scales(src, name):
            t = keep.tile([P, TOKENS], U8, name=name, align_bytes=256)
            nc.vector.memset(t[:].bitcast(I32), 0)
            for quad in range(4):
                nc.sync.dma_start(
                    t[32 * quad : 32 * quad + 4, :].bitcast(I32), src[0, 4 * quad : 4 * quad + 4, :].bitcast(I32)
                )
            return t

        def zeros(name, tag):
            t = keep.tile([P, TOKENS], F32, name=name, tag=tag, align_bytes=64)
            nc.vector.memset(t[:], 0.0)
            return t

        def grouped_views(raw, name):
            grouped = keep.tile([P, ROWS, PACK], BF16, name=name + "_bf", tag=name + "_bf", align_bytes=64)
            dst = grouped[:].rearrange("p (c i) t -> p c t i", i=4)
            src = raw[:].rearrange("p t (c i) -> p c t i", i=4)
            return grouped, dst, src

        def quantise(grouped, name):
            codes = keep.tile([P, ROWS], U32, name=name + "_codes", align_bytes=256)
            plane = keep.tile([P, ROWS], U8, name=name + "_plane", align_bytes=64)
            nc.vector.quantize_mx(codes[:].bitcast(FP8X4), plane[:], grouped[:].rearrange("p w j -> p (w j)"))
            return codes, plane

        def scores(q, words, plane, fp4, col, width, bank):
            acc = psum.tile([P, width], F32, name="acc%d" % bank, tag="bank%d" % bank)
            if fp4:
                rhs = words[:, 2 * col : 2 * (col + width)].bitcast(FP4X4)
            else:
                rhs = words[:, col : col + width].bitcast(FP8X4)
            nc.tensor.matmul_mx(
                acc[:], lhsT=q[0][:].bitcast(FP8X4), lhsT_scale=q[1][:], rhs=rhs,
                rhs_scale=plane[:, col : col + width], start=True, stop=True,
            )
            return acc

        q2_raw = load_query(query2, "q2")
        arch_w = load_words4(arch_words, "arch_w")
        arch_s = load_scales(arch_scales, "arch_s")
        q1_raw = load_query(query, "q1")
        pick_c = load_list(offs3, "pick_c")
        put_c = load_list(offs4, "put_c")
        draft_w = load_words8(draft_words, "draft_w")
        draft_s = load_scales(draft_scales, "draft_s")
        pick_b = load_list(offs, "pick_b")
        put_b = load_list(offs2, "put_b")
        pref_w = load_words8(pref_words, "pref_w")
        pref_s = load_scales(pref_scales, "pref_s")
        pick_d = load_list(offs5, "pick_d")
        put_d = load_list(offs6, "put_d")
        cache_w = load_words4(cache_words, "cache_w")
        cache_s = load_scales(cache_scales, "cache_s")
        pick_out = load_list(offs7, "pick_out")
        f2 = zeros("f2", "f2")

        q2_bf, dst, src = grouped_views(q2_raw, "q2")
        nc.vector.tensor_copy(dst, src)
        q2 = quantise(q2_bf, "q2")
        q1_bf, dst, src = grouped_views(q1_raw, "q1")
        nc.scalar.activation(dst, src, COPY)

        c_sb = keep.tile([P, TOKENS], F32, name="c_sb")
        quarter = TOKENS // 4
        for i in range(4):
            acc = scores(q2, arch_w, arch_s, True, i * quarter, quarter, i)
            cols = c_sb[:, i * quarter : (i + 1) * quarter]
            if i % 2 == 0:
                nc.vector.tensor_copy(cols, acc[:])
            else:
                nc.scalar.copy(cols, acc[:])
        q1 = quantise(q1_bf, "q1")
        f1 = zeros("f1", "q2_bf")
        half_cols = LIST_COLS // 2
        for h in range(2):
            part = slice(h * half_cols, (h + 1) * half_cols)
            picked = keep.tile([P, SLOTS // 2], F32, name="picked_c%d" % h)
            nc.vector.tensor_copy(picked[:], c_sb[:].indirect(pick_c[:, part]))
            nc.scalar.activation(f2[:].indirect(put_c[:, part]), picked[:], COPY)

        def pick_scores(q, words, plane, pick, first_bank, name):
            sb = keep.tile([P, TOKENS], F32, name=name + "_sb", tag=name + "_sb", align_bytes=64)
            for i in range(2):
                acc = scores(q, words, plane, False, i * BANK, BANK, first_bank + i)
                nc.vector.tensor_copy(sb[:, i * BANK : (i + 1) * BANK], acc[:])
            picked = keep.tile([P, SLOTS], F32, name="picked_" + name)
            nc.vector.tensor_copy(picked[:], sb[:].indirect(pick[:]))
            return picked

        picked_b = pick_scores(q1, draft_w, draft_s, pick_b, 4, "b")
        nc.scalar.activation(f1[:].indirect(put_b[:]), picked_b[:], COPY)
        picked_d = pick_scores(q2, pref_w, pref_s, pick_d, 6, "d")
        f3 = zeros("f3", "b_sb")
        nc.scalar.activation(f3[:].indirect(put_d[:]), picked_d[:], COPY)

        a_banks = [scores(q1, cache_w, cache_s, True, i * BANK, BANK, i) for i in range(2)]

        m1 = keep.tile([P, TOKENS], F32, name="m1", tag="d_sb", align_bytes=64)
        nc.vector.tensor_tensor(m1[:], f1[:], f2[:], ALU.max)
        m2 = keep.tile([P, TOKENS], F32, name="m2")
        aa = keep.tile([P, TOKENS], F32, name="aa")
        for i in range(2):
            cols = slice(i * BANK, (i + 1) * BANK)
            nc.vector.tensor_tensor(m2[:, cols], m1[:, cols], f3[:, cols], ALU.min)
        for i in range(2):
            cols = slice(i * BANK, (i + 1) * BANK)
            nc.vector.tensor_tensor(aa[:, cols], a_banks[i][:], m2[:, cols], ALU.subtract)

        half = SLOTS // 2
        y0 = keep.tile([P, half], F32, name="y0")
        y1 = keep.tile([P, half], F32, name="y1")
        nc.vector.tensor_copy(y0[:], aa[:].indirect(pick_out[:, 0:half_cols]))
        nc.sync.dma_start(out[:, 0:half], y0[:])
        nc.scalar.activation(y1[:], aa[:].indirect(pick_out[:, half_cols:LIST_COLS]), COPY)
        nc.scalar.dma_start(out[:, half:SLOTS], y1[:])
